import numpy as np
import ml_dtypes


def mxq(x, axis, fmt="e4m3"):
    dtype, down = {"e4m3": (ml_dtypes.float8_e4m3fn, 7), "e5m2": (ml_dtypes.float8_e5m2, 14)}[fmt]
    v = np.moveaxis(np.asarray(x, np.float32).astype(ml_dtypes.bfloat16).astype(np.float64), axis, -1)
    blocks = v.reshape(v.shape[:-1] + (-1, 32))
    amax = np.abs(blocks).max(-1, keepdims=True)
    byte = np.maximum(np.where(amax > 0, np.frexp(amax)[1] - 1 + 127, 0) - down, 1)
    scale = np.exp2(byte - 127.0)
    codes = (blocks / scale).astype(np.float32).astype(dtype).astype(np.float64)
    return np.moveaxis((codes * scale).reshape(v.shape), -1, axis)


WIDE = False


def mx_kscale(k):
    if not WIDE:
        return np.ones(k)
    levels = np.array([10, -10, 5, -5, 0])
    if k % 512:
        return np.exp2(np.random.permutation(np.resize(levels, k // 32))).repeat(32)
    a = np.empty((k // 512, 16))
    for p in range(k // 512):
        a[p, :8] = np.random.permutation(np.resize(levels, 8))
        for g in range(8):
            far = levels[np.abs(levels - a[p, g]) >= 10]
            a[p, g + 8] = far[np.random.randint(len(far))]
    return np.exp2(a.ravel()).repeat(32)


BF16 = ml_dtypes.bfloat16


def bf(x):
    return np.asarray(x, np.float32).astype(BF16)


def f64(x):
    return np.asarray(x).astype(np.float64)


E2M1 = np.array([0.0, 0.5, 1.0, 1.5, 2.0, 3.0, 4.0, 6.0, -0.0, -0.5, -1.0, -1.5, -2.0, -3.0, -4.0, -6.0])


def pack_weight(w, fmt):
    k, n = w.shape
    w = f64(bf(w)).reshape(k // 32, 32, n)
    amax = np.abs(w).max(1)
    if fmt == "e4m3":
        byte = np.frexp(amax)[1] - 1 + 127 - 7
    else:
        mant, ex = np.frexp(amax / 6.0)
        byte = np.where(mant > 0.5, ex, ex - 1) + 127
    byte = np.clip(np.where(amax > 0, byte, 1), 1, 254)
    scaled = (w * np.exp2(127.0 - byte)[:, None, :]).reshape(k, n).astype(np.float32)
    by_word = np.ascontiguousarray(scaled.reshape(k // 512, 128, 4, n).transpose(0, 1, 3, 2))
    if fmt == "e4m3":
        words = by_word.astype(ml_dtypes.float8_e4m3fn).view(np.uint8)
    else:
        c = by_word.astype(ml_dtypes.float4_e2m1fn).view(np.uint8) & 0xF
        words = c[..., 0::2] | (c[..., 1::2] << 4)
    return np.ascontiguousarray(words), np.ascontiguousarray(byte.astype(np.uint8).reshape(k // 512, 16, n))


def unpack_weight(words, scales, fmt):
    g, p, n, _ = words.shape
    if fmt == "e4m3":
        vals = np.ascontiguousarray(words).view(ml_dtypes.float8_e4m3fn).astype(np.float64)
    else:
        nib = np.empty((g, p, n, 4), np.uint8)
        nib[..., 0::2] = words & 0xF
        nib[..., 1::2] = words >> 4
        vals = E2M1[nib]
    vals = vals * np.repeat(np.exp2(scales.astype(np.float64) - 127.0), 8, axis=1)[..., None]
    return vals.transpose(0, 1, 3, 2).reshape(g * 512, n)

E4M3FN = np.array([(-1.0 if i & 128 else 1.0) * ((1.0 + (i & 7) / 8.0) * 2.0 ** (((i >> 3) & 15) - 7) if i & 120 else (i & 7) * 2.0 ** -9) for i in range(256)])


def e4m3fn_bytes(y):
    return np.clip(np.asarray(y, np.float64), -448.0, 448.0).astype(np.float32).astype(ml_dtypes.float8_e4m3fn).view(np.uint8)


def e4m3fn_values(b):
    return E4M3FN[b]


T, D, R, N = 1024, 1024, 512, 1024


def masked_coupling(m, pattern):
    return np.where(pattern < 0.25, m, np.zeros_like(m))


def draw0():
    s, r, t = mx_kscale(D), mx_kscale(R), mx_kscale(R)
    x = bf(np.random.standard_normal((T, D)) * s)
    w0_words, w0_scales = pack_weight(np.random.standard_normal((D, N)) / np.sqrt(D) / s[:, None], "e4m3")
    u_words, u_scales = pack_weight(np.random.standard_normal((D, R)) / np.sqrt(D) / s[:, None] * t, "e4m3")
    m = bf(np.random.standard_normal((R, R)) * 2.0 / np.sqrt(R) * r / t[:, None])
    pattern = bf(np.random.uniform(0.0, 1.0, (R, R)))
    vt_words, vt_scales = pack_weight(np.random.standard_normal((R, N)) / np.sqrt(R) / r[:, None], "e4m3")
    return {"x": x,
            "w0_words": w0_words, "w0_scales": w0_scales,
            "u_words": u_words, "u_scales": u_scales,
            "m": m,
            "pattern": pattern,
            "vt_words": vt_words, "vt_scales": vt_scales}


def core(x, w0_words, w0_scales, u_words, u_scales, m, pattern, vt_words, vt_scales):
    xq = mxq(f64(x), 1, "e4m3")
    ms = masked_coupling(f64(m), f64(pattern))
    n = mxq(ms, 1, "e4m3") @ unpack_weight(vt_words, vt_scales, "e4m3")
    h = xq @ unpack_weight(u_words, u_scales, "e4m3")
    d = mxq(h, 1, "e4m3") @ mxq(n, 0, "e4m3")
    b = xq @ unpack_weight(w0_words, w0_scales, "e4m3")
    y = b + d
    return y


def setup_inputs():
    drawn = draw0()
    full = np.asarray(drawn['x']).astype(np.float64)
    scale = (np.abs(full).reshape(1024, 8, 128).max(axis=(2,)) / 448.0).astype(np.float32)
    given = {}
    for key, value in drawn.items():
        if key == 'x':
            given['x_bytes'] = e4m3fn_bytes(full / np.repeat(scale.astype(np.float64), 128, axis=1))
            given['x_scale'] = scale
        else:
            given[key] = value
    return given


def reference(x_bytes, x_scale, w0_words, w0_scales, u_words, u_scales, m, pattern, vt_words, vt_scales):
    return core(e4m3fn_values(x_bytes) * np.repeat(x_scale.astype(np.float64), 128, axis=1), w0_words, w0_scales, u_words, u_scales, m, pattern, vt_words, vt_scales)

@@ -1,0 +1,316 @@
+from contextlib import ExitStack
+
+import concourse.mybir as mybir
+from concourse.masks import make_identity
+
+T, D, R, N = 1024, 1024, 512, 1024
+FLOPS = 2 * (R * R * N + T * D * R + T * R * N + T * D * N)
+
+P = 128
+F32 = mybir.dt.float32
+BF16 = mybir.dt.bfloat16
+I32 = mybir.dt.int32
+U32 = mybir.dt.uint32
+U8 = mybir.dt.uint8
+FP8 = mybir.dt.float8_e4m3fn
+X4 = mybir.dt.float8_e4m3fn_x4
+ALU = mybir.AluOpType
+ACT = mybir.ActivationFunctionType
+
+ORDER = (
+    "Wa.0.v Wb.0.s Ma.0.- Wb.1.s T.0.- Wa.1.v C.0.s Ma.1.- Mb.0.- T.1.- Mb.1.- Tm.0.- C.1.s Q.0.- UP.0.- "
+    "Tm.1.- Cm.0.s Cm.1.s Q.1.- H.0.- Qm.0.- H.1.- D.0.v N.0.- Wb.2.v I.0.- N.1.- Wa.2.s CN.0.v D.1.s "
+    "N.2.- CN.1.v N.3.- Wa.3.s N.4.- Wb.3.v N.5.- CN.2.s N.6.- Wa.4.v N.7.- T.2.- CN.3.s Wb.4.v CN.4.s "
+    "Wa.5.s Wb.5.v C.2.v CN.5.s T.3.- CN.6.s QN.0.- T.4.- T.5.- QN.1.- Q.2.- I.1.- CN.7.s Wa.6.v B.0.- "
+    "QN.2.- QN.3.- H.2.- C.3.s E.0.- Q.3.- B.1.- D.2.v Ob.0.s E.1.- Oa.0.v I.2.- H.3.- C.4.s Wb.6.v C.5.v "
+    "Q.4.- B.2.- E.2.- H.4.- Ob.1.s Wb.7.s Q.5.- Wa.7.v Oa.1.s D.3.v I.3.- Ob.2.v T.6.- Oa.2.v T.7.- "
+    "C.6.s D.4.s H.5.- B.3.- I.4.- D.5.s Q.6.- C.7.s I.5.- E.3.- Q.7.- B.4.- Oa.3.s Ob.3.v H.6.- D.6.v "
+    "I.6.- E.4.- Oa.4.s H.7.- B.5.- E.5.- Ob.4.s D.7.s Oa.5.s B.6.- I.7.- E.6.- B.7.- Ob.5.s E.7.- Oa.6.v "
+    "Ob.6.s Oa.7.s Ob.7.v"
+)
+
+
+def tile_svftrandompatternsingularcoupling_d1p_kernel(
+    tc, x_bytes, x_scale, w0_words, w0_scales, u_words, u_scales, m, pattern, vt_words, vt_scales, out
+):
+    nc = tc.nc
+    with ExitStack() as ctx:
+        keep = ctx.enter_context(tc.tile_pool(name="keep", bufs=1))
+        work = ctx.enter_context(tc.tile_pool(name="work", bufs=4))
+        psum = ctx.enter_context(tc.psum_pool(name="psum", bufs=1))
+
+        xb = keep.tile([P, 8, D], U8, align_bytes=64, name="xb")
+        xs = keep.tile([P, 64], F32, align_bytes=64, name="xs")
+        pat = keep.tile([P, 4, R], BF16, align_bytes=64, name="pat")
+        mt = keep.tile([P, 4, R], BF16, align_bytes=64, name="mt")
+        msk = keep.tile([P, 4, R], BF16, align_bytes=64, name="msk")
+        uw = keep.tile([P, 2, R], U32, align_bytes=64, name="uw")
+        up = keep.tile([P, 2, R], U32, align_bytes=64, name="up")
+        us = keep.tile([P, R], U8, align_bytes=64, name="us")
+        usp = keep.tile([P, R], U8, align_bytes=64, name="usp")
+        vw = keep.tile([P, N], U32, align_bytes=64, name="vw")
+        vs = keep.tile([P, N], U8, align_bytes=64, name="vs")
+        ww = keep.tile([P, 2, N], U32, align_bytes=64, name="ww")
+        ws = keep.tile([P, N], U8, align_bytes=64, name="ws")
+        ident = keep.tile([P, P], F32, align_bytes=64, name="ident")
+        pident = keep.tile([P, P], F32, align_bytes=64, name="pident")
+        msb = keep.tile([P, 2048], BF16, align_bytes=64, name="msb")
+        msq = keep.tile([P, R], U32, align_bytes=64, name="msq")
+        mss = keep.tile([P, R], U8, align_bytes=64, name="mss")
+        nb = keep.tile([P, 4 * N], BF16, align_bytes=64, name="nb")
+        nq = keep.tile([P, N], U32, align_bytes=64, name="nq")
+        nsc = keep.tile([P, N], U8, align_bytes=64, name="nsc")
+        xq = keep.tile([P, 8, 256], U32, align_bytes=64, name="xq")
+        xsc = keep.tile([P, 8, 256], U8, align_bytes=64, name="xsc")
+
+        ctx.enter_context(tc.manual_schedule())
+
+        x_rows = x_bytes.rearrange("(p i) k -> p i k", i=8)
+        m_rows = m.rearrange("(p a) k -> p a k", a=4)
+        p_rows = pattern.rearrange("(p a) k -> p a k", a=4)
+        out_rows = out.rearrange("(p i) n -> p i n", i=8)
+        u_src = u_words.rearrange("g p n t -> p g (n t)").bitcast(I32)
+        w_src = w0_words.rearrange("g p n t -> p g (n t)").bitcast(I32)
+        v_src = vt_words[0].rearrange("p n t -> p (n t)").bitcast(I32)
+
+        def load_x(i, count):
+            nc.sync.dma_start(out=xb[:, i : i + count, :], in_=x_rows[:, i : i + count, :])
+
+        def load_scales(engine, tile, scales, rows):
+            for q in range(4):
+                src = scales[:, 4 * q : 4 * q + 4, :] if rows == 8 else scales[0, 4 * q : 4 * q + 4, :]
+                engine.dma_start(out=tile[32 * q : 32 * q + rows, :].bitcast(I32), in_=src.bitcast(I32))
+
+        make_identity(nc, ident[:])
+        nc.gpsimd.tensor_copy(
+            out=pident[:].rearrange("p (t q b) -> p t q b", t=4, q=16),
+            in_=ident[:].rearrange("p (q t b) -> p t q b", q=16, t=4),
+        )
+        nc.vector.memset(us[:].bitcast(I32), 0)
+        nc.vector.memset(vs[:].bitcast(I32), 0)
+        nc.vector.memset(ws[:].bitcast(I32), 0)
+        nc.sync.dma_start(out=xs[:], in_=x_scale.rearrange("(p i) j -> p (i j)", i=8))
+        load_x(0, 1)
+        load_x(1, 1)
+        load_scales(nc.scalar, us, u_scales, 8)
+        for a in (0, 2):
+            nc.sync.dma_start(out=pat[:, a : a + 2, :], in_=p_rows[:, a : a + 2, :])
+            nc.sync.dma_start(out=mt[:, a : a + 2, :], in_=m_rows[:, a : a + 2, :])
+        load_scales(nc.sync, vs, vt_scales, 4)
+        load_scales(nc.gpsimd, ws, w0_scales, 8)
+        nc.sync.dma_start(out=uw[:].bitcast(I32), in_=u_src)
+        nc.sync.dma_start(out=vw[:].bitcast(I32), in_=v_src)
+        load_x(2, 2)
+        for h in (0, 1):
+            nc.sync.dma_start(out=ww[:, :, 512 * h : 512 * h + 512].bitcast(I32), in_=w_src[:, :, 512 * h : 512 * h + 512])
+        load_x(4, 2)
+        load_x(6, 2)
+
+        live = {}
+        ring = []
+
+        def bank():
+            ring.append(0)
+            return psum.tile([P, 512], F32, tag="bank%d" % (len(ring) % 8), name="bank")
+
+        def widen(i, half, eng):
+            if ("xw", i) not in live:
+                live["xw", i] = work.tile([P, D], BF16, align_bytes=64, name="xw")
+            xw = live["xw", i]
+            for j in range(4 * half, 4 * half + 4):
+                src = xb[:, i, 128 * j : 128 * j + 128].bitcast(FP8)
+                dst = xw[:, 128 * j : 128 * j + 128]
+                sc = xs[:, 8 * i + j : 8 * i + j + 1]
+                if eng == "v":
+                    nc.vector.tensor_scalar(out=dst, in0=src, scalar1=sc, scalar2=None, op0=ALU.mult)
+                else:
+                    nc.scalar.activation(out=dst, in_=src, func=ACT.Copy, scale=sc)
+
+        def turn_x(i):
+            tr = bank()
+            live["tr", i] = tr
+            words = live["xw", i][:].bitcast(F32)
+            for g in (0, 1):
+                for u in (0, 1):
+                    c = 128 * (2 * g + u)
+                    nc.tensor.transpose(tr[:, c : c + 128], words[:, 256 * g + u : 256 * g + 256 : 2], ident[:])
+
+        def copy(eng, dst, src):
+            if eng == "v":
+                nc.vector.tensor_copy(out=dst, in_=src)
+            else:
+                nc.scalar.copy(out=dst, in_=src)
+
+        def copy_x(i, eng):
+            xg = work.tile([P, D], BF16, align_bytes=64, name="xg")
+            live["xg", i] = xg
+            copy(
+                eng,
+                xg[:].bitcast(F32).rearrange("p (g c u) -> p g c u", g=2, u=2),
+                live["tr", i][:].rearrange("p (g u c) -> p g c u", g=2, u=2),
+            )
+
+        def quant_x(i):
+            nc.vector.quantize_mx(out=xq[:, i, :].bitcast(X4), scales=xsc[:, i, :], in_=live["xg", i][:])
+
+        def permute_u():
+            for g in (0, 1):
+                nc.vector.tensor_copy(
+                    out=up[:, g, :].bitcast(I32).rearrange("p (t q j) -> p t q j", t=4, q=16),
+                    in_=uw[:, g, :].bitcast(I32).rearrange("p (q t j) -> p t q j", q=16, t=4),
+                )
+            nc.vector.tensor_copy(
+                out=usp[:].bitcast(I32).rearrange("p (t q j) -> p t q j", t=4, q=16),
+                in_=us[:].bitcast(I32).rearrange("p (q t j) -> p t q j", q=16, t=4),
+            )
+
+        def mask_a(h):
+            a = slice(2 * h, 2 * h + 2)
+            nc.vector.tensor_scalar(out=msk[:, a, :], in0=pat[:, a, :], scalar1=0.25, scalar2=None, op0=ALU.is_lt)
+
+        def mask_b(h):
+            a = slice(2 * h, 2 * h + 2)
+            nc.vector.tensor_tensor(out=msk[:, a, :], in0=msk[:, a, :], in1=mt[:, a, :], op=ALU.mult)
+
+        def turn_m(h):
+            tr = bank()
+            live["trm", h] = tr
+            for e in (0, 1):
+                words = msk[:, 2 * h + e, :].bitcast(F32)
+                for u in (0, 1):
+                    c = 128 * (2 * e + u)
+                    nc.tensor.transpose(tr[:, c : c + 128], words[:, u:256:2], pident[:])
+
+        def copy_m(h, eng):
+            dst = msb[:].bitcast(F32).rearrange("p (c a u) -> p c a u", a=4, u=2)[:, :, 2 * h : 2 * h + 2, :]
+            copy(eng, dst, live["trm", h][:].rearrange("p (a u c) -> p c a u", a=2, u=2))
+
+        def quant_m():
+            nc.vector.quantize_mx(out=msq[:].bitcast(X4), scales=mss[:], in_=msb[:])
+
+        def mm_n(c):
+            acc = bank()
+            live["n", c] = acc
+            cols = slice(128 * c, 128 * c + 128)
+            for t in range(4):
+                nc.tensor.matmul_mx(
+                    out=acc[:, 128 * t : 128 * t + 128],
+                    lhsT=msq[:, 128 * t : 128 * t + 128].bitcast(X4),
+                    lhsT_scale=mss[:, 128 * t : 128 * t + 128],
+                    rhs=vw[:, cols].bitcast(X4),
+                    rhs_scale=vs[:, cols],
+                    start=True,
+                    stop=True,
+                )
+
+        def copy_n(c, eng):
+            copy(
+                eng,
+                nb[:, 512 * c : 512 * c + 512].rearrange("p (n t) -> p n t", t=4),
+                live["n", c][:].rearrange("p (t n) -> p n t", t=4),
+            )
+
+        def quant_n(h):
+            nc.vector.quantize_mx(
+                out=nq[:, 256 * h : 256 * h + 256].bitcast(X4),
+                scales=nsc[:, 256 * h : 256 * h + 256],
+                in_=nb[:, 1024 * h : 1024 * h + 1024],
+            )
+
+        def mm_h(i):
+            acc = bank()
+            live["h", i] = acc
+            for t in range(4):
+                for g in (0, 1):
+                    nc.tensor.matmul_mx(
+                        out=acc[:, 128 * t : 128 * t + 128],
+                        lhsT=up[:, g, 128 * t : 128 * t + 128].bitcast(X4),
+                        lhsT_scale=usp[4 * g : P, 128 * t : 128 * t + 128],
+                        rhs=xq[:, i, 128 * g : 128 * g + 128].bitcast(X4),
+                        rhs_scale=xsc[:, i, 128 * g : 128 * g + 128],
+                        start=(g == 0),
+                        stop=(g == 1),
+                    )
+
+        def copy_h(i, eng):
+            hb = work.tile([P, 512], BF16, align_bytes=64, name="hb")
+            live["hb", i] = hb
+            copy(eng, hb[:].rearrange("p (n t) -> p n t", t=4), live["h", i][:].rearrange("p (t n) -> p n t", t=4))
+
+        def quant_h(i):
+            hq = work.tile([P, P], U32, align_bytes=64, name="hq", bufs=8)
+            hs = work.tile([P, P], U8, align_bytes=64, name="hs", bufs=8)
+            live["hq", i] = (hq, hs)
+            nc.vector.quantize_mx(out=hq[:].bitcast(X4), scales=hs[:], in_=live["hb", i][:])
+
+        def mm_b(i):
+            o0 = bank()
+            o1 = bank()
+            live["o", i] = (o0, o1)
+            live["osb", i] = work.tile([P, N], F32, align_bytes=64, name="osb")
+            for g in (0, 1):
+                for h in (0, 1):
+                    nc.tensor.matmul_mx(
+                        out=live["o", i][h][:],
+                        lhsT=xq[:, i, 128 * g : 128 * g + 128].bitcast(X4),
+                        lhsT_scale=xsc[:, i, 128 * g : 128 * g + 128],
+                        rhs=ww[:, g, 512 * h : 512 * h + 512].bitcast(X4),
+                        rhs_scale=ws[4 * g : P, 512 * h : 512 * h + 512],
+                        start=(g == 0),
+                        stop=False,
+                    )
+
+        def mm_d(i):
+            hq, hs = live["hq", i]
+            for h in (0, 1):
+                nc.tensor.matmul_mx(
+                    out=live["o", i][h][:],
+                    lhsT=hq[:].bitcast(X4),
+                    lhsT_scale=hs[:],
+                    rhs=nq[:, 512 * h : 512 * h + 512].bitcast(X4),
+                    rhs_scale=nsc[:, 512 * h : 512 * h + 512],
+                    start=False,
+                    stop=True,
+                )
+
+        stored = []
+
+        def finish(i, h, eng):
+            osb = live["osb", i]
+            acc = live["o", i][h]
+            if i < 7:
+                copy(eng, osb[:, 512 * h : 512 * h + 512], acc[:])
+                stored.append(i)
+                if len([j for j in stored if j == i]) == 2:
+                    nc.sync.dma_start(out=out_rows[:, i, :], in_=osb[:])
+            else:
+                copy("s", osb[:, 512 * h : 512 * h + 256], acc[:, 0:256])
+                copy("v", osb[:, 512 * h + 256 : 512 * h + 512], acc[:, 256:512])
+                nc.sync.dma_start(out=out_rows[:, i, 512 * h : 512 * h + 512], in_=osb[:, 512 * h : 512 * h + 512])
+
+        steps = {
+            "Wa": lambda i, e: widen(i, 0, e),
+            "Wb": lambda i, e: widen(i, 1, e),
+            "T": lambda i, e: turn_x(i),
+            "C": copy_x,
+            "Q": lambda i, e: quant_x(i),
+            "UP": lambda i, e: permute_u(),
+            "Ma": lambda i, e: mask_a(i),
+            "Mb": lambda i, e: mask_b(i),
+            "Tm": lambda i, e: turn_m(i),
+            "Cm": copy_m,
+            "Qm": lambda i, e: quant_m(),
+            "N": lambda i, e: mm_n(i),
+            "CN": copy_n,
+            "QN": lambda i, e: quant_n(i),
+            "H": lambda i, e: mm_h(i),
+            "D": copy_h,
+            "I": lambda i, e: quant_h(i),
+            "B": lambda i, e: mm_b(i),
+            "E": lambda i, e: mm_d(i),
+            "Oa": lambda i, e: finish(i, 0, e),
+            "Ob": lambda i, e: finish(i, 1, e),
+        }
+        for step in ORDER.split(" "):
+            kind, index, engine = step.split(".")
+            steps[kind](int(index), engine)

@@ -18,15 +18,15 @@ ALU = mybir.AluOpType
 ACT = mybir.ActivationFunctionType
 
 ORDER = (
-    "Wa.0.v Wb.0.s Ma.0.- Wb.1.s T.0.- Wa.1.v C.0.s Ma.1.- Mb.0.- T.1.- Mb.1.- Tm.0.- C.1.s Q.0.- UP.0.- "
-    "Tm.1.- Cm.0.s Cm.1.s Q.1.- H.0.- Qm.0.- H.1.- D.0.v N.0.- Wb.2.v I.0.- N.1.- Wa.2.s CN.0.v D.1.s "
-    "N.2.- CN.1.v N.3.- Wa.3.s N.4.- Wb.3.v N.5.- CN.2.s N.6.- Wa.4.v N.7.- T.2.- CN.3.s Wb.4.v CN.4.s "
-    "Wa.5.s Wb.5.v C.2.v CN.5.s T.3.- CN.6.s QN.0.- T.4.- T.5.- QN.1.- Q.2.- I.1.- CN.7.s Wa.6.v B.0.- "
-    "QN.2.- QN.3.- H.2.- C.3.s E.0.- Q.3.- B.1.- D.2.v Ob.0.s E.1.- Oa.0.v I.2.- H.3.- C.4.s Wb.6.v C.5.v "
-    "Q.4.- B.2.- E.2.- H.4.- Ob.1.s Wb.7.s Q.5.- Wa.7.v Oa.1.s D.3.v I.3.- Ob.2.v T.6.- Oa.2.v T.7.- "
-    "C.6.s D.4.s H.5.- B.3.- I.4.- D.5.s Q.6.- C.7.s I.5.- E.3.- Q.7.- B.4.- Oa.3.s Ob.3.v H.6.- D.6.v "
-    "I.6.- E.4.- Oa.4.s H.7.- B.5.- E.5.- Ob.4.s D.7.s Oa.5.s B.6.- I.7.- E.6.- B.7.- Ob.5.s E.7.- Oa.6.v "
-    "Ob.6.s Oa.7.s Ob.7.v"
+    "Wb.0.v Wa.0.s Wb.1.v T.0.- Ma.0.- Wa.1.s Mb.0.- Ma.1.- T.1.- C.0.s Mb.1.- Tm.0.- Q.0.- Wb.2.s Wa.2.v "
+    "Tm.1.- T.2.- C.1.s Cm.0.s Cm.1.s Wa.3.v Wb.3.v UP.0.- C.2.s T.3.- H.0.- Qm.0.- C.3.s N.0.- Q.1.- "
+    "Q.2.- D.0.v N.1.- Wb.4.v N.2.- CN.0.s Q.3.- N.3.- CN.1.s CN.2.v N.4.- Wa.4.v H.1.- H.2.- CN.3.s "
+    "H.3.- N.5.- N.6.- D.1.v CN.4.s I.0.- QN.0.- CN.5.v QN.1.- Wb.5.v D.2.s D.3.s CN.6.s N.7.- Wa.5.v "
+    "B.0.- B.1.- Wa.6.v CN.7.s QN.2.- Wb.6.v T.4.- T.5.- QN.3.- I.1.- E.0.- C.4.s E.1.- C.5.v Wa.7.v "
+    "Ob.0.s Q.4.- Oa.0.s B.2.- I.2.- Ob.1.s Wb.7.v E.2.- Oa.1.v H.4.- Oa.2.s Q.5.- I.3.- Ob.2.s T.6.- "
+    "D.4.v T.7.- B.3.- E.3.- H.5.- B.4.- I.4.- C.6.s Q.6.- D.5.v I.5.- Ob.3.v E.4.- B.5.- Oa.3.s Oa.4.v "
+    "C.7.v E.5.- H.6.- Ob.4.s D.6.s Ob.5.v Q.7.- Oa.5.s B.6.- H.7.- I.6.- E.6.- D.7.s B.7.- Oa.6.s I.7.- "
+    "E.7.- Ob.6.v Oa.7.s Ob.7.v"
 )
 
 
@@ -96,11 +96,11 @@ def tile_svftrandompatternsingularcoupling_d1p_kernel(
         for a in (0, 2):
             nc.sync.dma_start(out=pat[:, a : a + 2, :], in_=p_rows[:, a : a + 2, :])
             nc.sync.dma_start(out=mt[:, a : a + 2, :], in_=m_rows[:, a : a + 2, :])
+        load_x(2, 2)
         load_scales(nc.sync, vs, vt_scales, 4)
         load_scales(nc.gpsimd, ws, w0_scales, 8)
         nc.sync.dma_start(out=uw[:].bitcast(I32), in_=u_src)
         nc.sync.dma_start(out=vw[:].bitcast(I32), in_=v_src)
-        load_x(2, 2)
         for h in (0, 1):
             nc.sync.dma_start(out=ww[:, :, 512 * h : 512 * h + 512].bitcast(I32), in_=w_src[:, :, 512 * h : 512 * h + 512])
         load_x(4, 2)
@@ -116,15 +116,23 @@ def tile_svftrandompatternsingularcoupling_d1p_kernel(
         def widen(i, half, eng):
             if ("xw", i) not in live:
                 live["xw", i] = work.tile([P, D], BF16, align_bytes=64, name="xw")
+            live["split", i, half] = eng == "v"
             xw = live["xw", i]
-            for j in range(4 * half, 4 * half + 4):
+            pairs = xw[:, 512 * half : 512 * half + 512].rearrange("p (u c e) -> p c u e", u=2, e=2)
+            for b in range(4):
+                j = 4 * half + b
                 src = xb[:, i, 128 * j : 128 * j + 128].bitcast(FP8)
-                dst = xw[:, 128 * j : 128 * j + 128]
                 sc = xs[:, 8 * i + j : 8 * i + j + 1]
                 if eng == "v":
-                    nc.vector.tensor_scalar(out=dst, in0=src, scalar1=sc, scalar2=None, op0=ALU.mult)
+                    nc.vector.tensor_scalar(
+                        out=pairs[:, 32 * b : 32 * b + 32, :, :],
+                        in0=src.rearrange("p (c u e) -> p c u e", u=2, e=2),
+                        scalar1=sc,
+                        scalar2=None,
+                        op0=ALU.mult,
+                    )
                 else:
-                    nc.scalar.activation(out=dst, in_=src, func=ACT.Copy, scale=sc)
+                    nc.scalar.activation(out=xw[:, 128 * j : 128 * j + 128], in_=src, func=ACT.Copy, scale=sc)
 
         def turn_x(i):
             tr = bank()
@@ -133,7 +141,11 @@ def tile_svftrandompatternsingularcoupling_d1p_kernel(
             for g in (0, 1):
                 for u in (0, 1):
                     c = 128 * (2 * g + u)
-                    nc.tensor.transpose(tr[:, c : c + 128], words[:, 256 * g + u : 256 * g + 256 : 2], ident[:])
+                    if live["split", i, g]:
+                        src = words[:, 256 * g + 128 * u : 256 * g + 128 * u + 128]
+                    else:
+                        src = words[:, 256 * g + u : 256 * g + 256 : 2]
+                    nc.tensor.transpose(tr[:, c : c + 128], src, ident[:])
 
         def copy(eng, dst, src):
             if eng == "v":

@@ -18,15 +18,16 @@ ALU = mybir.AluOpType
 ACT = mybir.ActivationFunctionType
 
 ORDER = (
-    "Wb.0.v Wa.0.s Wb.1.v T.0.- Ma.0.- Wa.1.s Mb.0.- Ma.1.- T.1.- C.0.s Mb.1.- Tm.0.- Q.0.- Wb.2.s Wa.2.v "
-    "Tm.1.- T.2.- C.1.s Cm.0.s Cm.1.s Wa.3.v Wb.3.v UP.0.- C.2.s T.3.- H.0.- Qm.0.- C.3.s N.0.- Q.1.- "
-    "Q.2.- D.0.v N.1.- Wb.4.v N.2.- CN.0.s Q.3.- N.3.- CN.1.s CN.2.v N.4.- Wa.4.v H.1.- H.2.- CN.3.s "
-    "H.3.- N.5.- N.6.- D.1.v CN.4.s I.0.- QN.0.- CN.5.v QN.1.- Wb.5.v D.2.s D.3.s CN.6.s N.7.- Wa.5.v "
-    "B.0.- B.1.- Wa.6.v CN.7.s QN.2.- Wb.6.v T.4.- T.5.- QN.3.- I.1.- E.0.- C.4.s E.1.- C.5.v Wa.7.v "
-    "Ob.0.s Q.4.- Oa.0.s B.2.- I.2.- Ob.1.s Wb.7.v E.2.- Oa.1.v H.4.- Oa.2.s Q.5.- I.3.- Ob.2.s T.6.- "
-    "D.4.v T.7.- B.3.- E.3.- H.5.- B.4.- I.4.- C.6.s Q.6.- D.5.v I.5.- Ob.3.v E.4.- B.5.- Oa.3.s Oa.4.v "
-    "C.7.v E.5.- H.6.- Ob.4.s D.6.s Ob.5.v Q.7.- Oa.5.s B.6.- H.7.- I.6.- E.6.- D.7.s B.7.- Oa.6.s I.7.- "
-    "E.7.- Ob.6.v Oa.7.s Ob.7.v"
+    "Wa.0.s Wb.0.v Wa.1.v Wb.1.s T.0.- C.0.s T.1.- Ma.0.- Mb.0.- Ma.1.- Mb.1.- C.1.v Tm.0.- Tm.1.- Q.0.- "
+    "Q.1.- Wb.2.v Wa.2.v Wa.3.v Ba.0.- Cm.0.s Ba.1.- UP.0.- T.2.- Cm.1.s H.0.- C.2.s Qm.0.- D.0.v N.0.- "
+    "Wb.3.v N.1.- Wa.4.v Q.2.- N.2.- Bb.0.- Wb.4.v CN.0.s H.1.- N.3.- CN.1.s I.0.- QN.0.- T.3.- Wb.5.v "
+    "CN.2.s D.1.s T.4.- N.4.- Wb.6.v CN.3.s Wa.5.v Bb.1.- C.3.s N.5.- C.4.s Wb.7.v H.2.- QN.1.- N.6.- "
+    "CN.4.s Wa.6.v I.1.- Ea.0.- N.7.- Q.3.- D.2.v Wa.7.v CN.5.s Q.4.- QN.2.- H.3.- T.5.- CN.6.s T.6.- "
+    "D.3.v I.2.- CN.7.s T.7.- Oa.0.s QN.3.- I.3.- C.5.v Ea.1.- C.6.s Ba.2.- H.4.- Q.5.- Eb.0.- C.7.v "
+    "Oa.1.s D.4.v Ea.2.- Q.6.- Ba.3.- I.4.- Eb.1.- Oa.2.v Ob.0.s Ea.3.- Bb.2.- Eb.2.- Ob.1.s H.5.- H.6.- "
+    "D.5.s Q.7.- Bb.3.- Eb.3.- H.7.- Ba.4.- Oa.3.s Ob.2.s I.5.- Ea.4.- Bb.4.- Eb.4.- Ob.3.s Ob.4.v Bb.5.- "
+    "D.6.s Oa.4.s Eb.5.- Ba.5.- I.6.- Bb.6.- Eb.6.- D.7.v Ea.5.- Ba.6.- I.7.- Ob.5.s Ea.6.- Bb.7.- Ob.6.v "
+    "Oa.5.s Oa.6.v Eb.7.- Ob.7.s Ba.7.- Ea.7.- Oa.7.v"
 )
 
 
@@ -96,22 +97,22 @@ def tile_svftrandompatternsingularcoupling_d1p_kernel(
         for a in (0, 2):
             nc.sync.dma_start(out=pat[:, a : a + 2, :], in_=p_rows[:, a : a + 2, :])
             nc.sync.dma_start(out=mt[:, a : a + 2, :], in_=m_rows[:, a : a + 2, :])
+        load_scales(nc.sync, ws, w0_scales, 8)
+        nc.sync.dma_start(out=ww[:, :, 0:512].bitcast(I32), in_=w_src[:, :, 0:512])
         load_x(2, 2)
-        load_scales(nc.sync, vs, vt_scales, 4)
-        load_scales(nc.gpsimd, ws, w0_scales, 8)
         nc.sync.dma_start(out=uw[:].bitcast(I32), in_=u_src)
+        load_scales(nc.sync, vs, vt_scales, 4)
         nc.sync.dma_start(out=vw[:].bitcast(I32), in_=v_src)
-        for h in (0, 1):
-            nc.sync.dma_start(out=ww[:, :, 512 * h : 512 * h + 512].bitcast(I32), in_=w_src[:, :, 512 * h : 512 * h + 512])
+        nc.sync.dma_start(out=ww[:, :, 512:1024].bitcast(I32), in_=w_src[:, :, 512:1024])
         load_x(4, 2)
         load_x(6, 2)
 
         live = {}
-        ring = []
+        turn = {"r": 0, "o": 0}
 
-        def bank():
-            ring.append(0)
-            return psum.tile([P, 512], F32, tag="bank%d" % (len(ring) % 8), name="bank")
+        def bank(ring):
+            turn[ring] = (turn[ring] + 1) % 4
+            return psum.tile([P, 512], F32, tag="%s%d" % (ring, turn[ring]), name="bank")
 
         def widen(i, half, eng):
             if ("xw", i) not in live:
@@ -135,7 +136,7 @@ def tile_svftrandompatternsingularcoupling_d1p_kernel(
                     nc.scalar.activation(out=xw[:, 128 * j : 128 * j + 128], in_=src, func=ACT.Copy, scale=sc)
 
         def turn_x(i):
-            tr = bank()
+            tr = bank("r")
             live["tr", i] = tr
             words = live["xw", i][:].bitcast(F32)
             for g in (0, 1):
@@ -185,7 +186,7 @@ def tile_svftrandompatternsingularcoupling_d1p_kernel(
             nc.vector.tensor_tensor(out=msk[:, a, :], in0=msk[:, a, :], in1=mt[:, a, :], op=ALU.mult)
 
         def turn_m(h):
-            tr = bank()
+            tr = bank("r")
             live["trm", h] = tr
             for e in (0, 1):
                 words = msk[:, 2 * h + e, :].bitcast(F32)
@@ -201,7 +202,7 @@ def tile_svftrandompatternsingularcoupling_d1p_kernel(
             nc.vector.quantize_mx(out=msq[:].bitcast(X4), scales=mss[:], in_=msb[:])
 
         def mm_n(c):
-            acc = bank()
+            acc = bank("r")
             live["n", c] = acc
             cols = slice(128 * c, 128 * c + 128)
             for t in range(4):
@@ -230,7 +231,7 @@ def tile_svftrandompatternsingularcoupling_d1p_kernel(
             )
 
         def mm_h(i):
-            acc = bank()
+            acc = bank("r")
             live["h", i] = acc
             for t in range(4):
                 for g in (0, 1):
@@ -255,50 +256,42 @@ def tile_svftrandompatternsingularcoupling_d1p_kernel(
             live["hq", i] = (hq, hs)
             nc.vector.quantize_mx(out=hq[:].bitcast(X4), scales=hs[:], in_=live["hb", i][:])
 
-        def mm_b(i):
-            o0 = bank()
-            o1 = bank()
-            live["o", i] = (o0, o1)
-            live["osb", i] = work.tile([P, N], F32, align_bytes=64, name="osb")
+        def mm_b(i, h):
+            acc = bank("o")
+            live["o", i, h] = acc
+            cols = slice(512 * h, 512 * h + 512)
             for g in (0, 1):
-                for h in (0, 1):
-                    nc.tensor.matmul_mx(
-                        out=live["o", i][h][:],
-                        lhsT=xq[:, i, 128 * g : 128 * g + 128].bitcast(X4),
-                        lhsT_scale=xsc[:, i, 128 * g : 128 * g + 128],
-                        rhs=ww[:, g, 512 * h : 512 * h + 512].bitcast(X4),
-                        rhs_scale=ws[4 * g : P, 512 * h : 512 * h + 512],
-                        start=(g == 0),
-                        stop=False,
-                    )
-
-        def mm_d(i):
-            hq, hs = live["hq", i]
-            for h in (0, 1):
                 nc.tensor.matmul_mx(
-                    out=live["o", i][h][:],
-                    lhsT=hq[:].bitcast(X4),
-                    lhsT_scale=hs[:],
-                    rhs=nq[:, 512 * h : 512 * h + 512].bitcast(X4),
-                    rhs_scale=nsc[:, 512 * h : 512 * h + 512],
-                    start=False,
-                    stop=True,
+                    out=acc[:],
+                    lhsT=xq[:, i, 128 * g : 128 * g + 128].bitcast(X4),
+                    lhsT_scale=xsc[:, i, 128 * g : 128 * g + 128],
+                    rhs=ww[:, g, cols].bitcast(X4),
+                    rhs_scale=ws[4 * g : P, cols],
+                    start=(g == 0),
+                    stop=False,
                 )
 
-        stored = []
+        def mm_d(i, h):
+            hq, hs = live["hq", i]
+            nc.tensor.matmul_mx(
+                out=live["o", i, h][:],
+                lhsT=hq[:].bitcast(X4),
+                lhsT_scale=hs[:],
+                rhs=nq[:, 512 * h : 512 * h + 512].bitcast(X4),
+                rhs_scale=nsc[:, 512 * h : 512 * h + 512],
+                start=False,
+                stop=True,
+            )
 
         def finish(i, h, eng):
-            osb = live["osb", i]
-            acc = live["o", i][h]
+            osb = work.tile([P, 512], F32, align_bytes=64, name="osb", bufs=6)
+            acc = live["o", i, h]
             if i < 7:
-                copy(eng, osb[:, 512 * h : 512 * h + 512], acc[:])
-                stored.append(i)
-                if len([j for j in stored if j == i]) == 2:
-                    nc.sync.dma_start(out=out_rows[:, i, :], in_=osb[:])
+                copy(eng, osb[:], acc[:])
             else:
-                copy("s", osb[:, 512 * h : 512 * h + 256], acc[:, 0:256])
-                copy("v", osb[:, 512 * h + 256 : 512 * h + 512], acc[:, 256:512])
-                nc.sync.dma_start(out=out_rows[:, i, 512 * h : 512 * h + 512], in_=osb[:, 512 * h : 512 * h + 512])
+                copy("s", osb[:, 0:256], acc[:, 0:256])
+                copy("v", osb[:, 256:512], acc[:, 256:512])
+            nc.sync.dma_start(out=out_rows[:, i, 512 * h : 512 * h + 512], in_=osb[:])
 
         steps = {
             "Wa": lambda i, e: widen(i, 0, e),
@@ -318,8 +311,10 @@ def tile_svftrandompatternsingularcoupling_d1p_kernel(
             "H": lambda i, e: mm_h(i),
             "D": copy_h,
             "I": lambda i, e: quant_h(i),
-            "B": lambda i, e: mm_b(i),
-            "E": lambda i, e: mm_d(i),
+            "Ba": lambda i, e: mm_b(i, 0),
+            "Bb": lambda i, e: mm_b(i, 1),
+            "Ea": lambda i, e: mm_d(i, 0),
+            "Eb": lambda i, e: mm_d(i, 1),
             "Oa": lambda i, e: finish(i, 0, e),
             "Ob": lambda i, e: finish(i, 1, e),
         }

@@ -18,16 +18,16 @@ ALU = mybir.AluOpType
 ACT = mybir.ActivationFunctionType
 
 ORDER = (
-    "Wa.0.s Wb.0.v Wa.1.v Wb.1.s T.0.- C.0.s T.1.- Ma.0.- Mb.0.- Ma.1.- Mb.1.- C.1.v Tm.0.- Tm.1.- Q.0.- "
-    "Q.1.- Wb.2.v Wa.2.v Wa.3.v Ba.0.- Cm.0.s Ba.1.- UP.0.- T.2.- Cm.1.s H.0.- C.2.s Qm.0.- D.0.v N.0.- "
-    "Wb.3.v N.1.- Wa.4.v Q.2.- N.2.- Bb.0.- Wb.4.v CN.0.s H.1.- N.3.- CN.1.s I.0.- QN.0.- T.3.- Wb.5.v "
-    "CN.2.s D.1.s T.4.- N.4.- Wb.6.v CN.3.s Wa.5.v Bb.1.- C.3.s N.5.- C.4.s Wb.7.v H.2.- QN.1.- N.6.- "
-    "CN.4.s Wa.6.v I.1.- Ea.0.- N.7.- Q.3.- D.2.v Wa.7.v CN.5.s Q.4.- QN.2.- H.3.- T.5.- CN.6.s T.6.- "
-    "D.3.v I.2.- CN.7.s T.7.- Oa.0.s QN.3.- I.3.- C.5.v Ea.1.- C.6.s Ba.2.- H.4.- Q.5.- Eb.0.- C.7.v "
-    "Oa.1.s D.4.v Ea.2.- Q.6.- Ba.3.- I.4.- Eb.1.- Oa.2.v Ob.0.s Ea.3.- Bb.2.- Eb.2.- Ob.1.s H.5.- H.6.- "
-    "D.5.s Q.7.- Bb.3.- Eb.3.- H.7.- Ba.4.- Oa.3.s Ob.2.s I.5.- Ea.4.- Bb.4.- Eb.4.- Ob.3.s Ob.4.v Bb.5.- "
-    "D.6.s Oa.4.s Eb.5.- Ba.5.- I.6.- Bb.6.- Eb.6.- D.7.v Ea.5.- Ba.6.- I.7.- Ob.5.s Ea.6.- Bb.7.- Ob.6.v "
-    "Oa.5.s Oa.6.v Eb.7.- Ob.7.s Ba.7.- Ea.7.- Oa.7.v"
+    "Wa.0.v Wb.0.s Wa.1.v Wb.1.v Ma.0.- T.0.- C.0.v Ma.1.- Mb.0.- Mb.1.- Q.0.- T.1.- Tm.0.- C.1.s Wb.2.s "
+    "Tm.1.- Cm.0.s Cm.1.s Wa.2.v Q.1.- Wb.3.v Ba.0.- T.2.- C.2.s Wa.3.v T.3.- Qm.0.- C.3.s UP.0.- Ba.1.- "
+    "N.0.- Q.2.- N.1.- N.2.- CN.0.s CN.1.v Q.3.- CN.2.s H.0.- N.3.- H.1.- D.0.s Wa.4.v Wa.5.v N.4.- "
+    "CN.3.s N.5.- QN.0.- QN.1.- I.0.- Wb.4.v D.1.s Wb.5.v Bb.0.- I.1.- H.2.- CN.4.s CN.5.s Wb.6.v Wa.6.v "
+    "H.3.- Wa.7.v N.6.- Ea.0.- Ea.1.- D.2.s Wb.7.v D.3.s CN.6.s N.7.- Ba.2.- T.4.- QN.2.- CN.7.s Oa.0.s "
+    "T.5.- I.2.- T.6.- QN.3.- C.4.s C.5.v Oa.1.s Q.4.- C.6.v T.7.- Ea.2.- Bb.1.- Eb.0.- Bb.2.- Eb.1.- "
+    "Ob.0.v H.4.- Oa.2.v Eb.2.- Ob.1.v Bb.3.- I.3.- Ba.3.- Eb.3.- D.4.s Q.5.- I.4.- Bb.4.- Ea.3.- Q.6.- "
+    "Ob.2.s H.5.- C.7.s Ba.4.- Oa.3.s Q.7.- Ob.3.v Eb.4.- D.5.v H.6.- Ea.4.- Bb.5.- Ba.5.- I.5.- Ob.4.v "
+    "D.6.s Eb.5.- H.7.- I.6.- Ba.6.- Oa.4.s D.7.s Ob.5.v Ea.5.- Bb.6.- Oa.5.s Ea.6.- Eb.6.- Ob.6.s Bb.7.- "
+    "I.7.- Oa.6.v Eb.7.- Ob.7.s Ba.7.- Ea.7.- Oa.7.v"
 )
 
 
@@ -37,7 +37,7 @@ def tile_svftrandompatternsingularcoupling_d1p_kernel(
     nc = tc.nc
     with ExitStack() as ctx:
         keep = ctx.enter_context(tc.tile_pool(name="keep", bufs=1))
-        work = ctx.enter_context(tc.tile_pool(name="work", bufs=4))
+        work = ctx.enter_context(tc.tile_pool(name="work", bufs=8))
         psum = ctx.enter_context(tc.psum_pool(name="psum", bufs=1))
 
         xb = keep.tile([P, 8, D], U8, align_bytes=64, name="xb")
@@ -82,6 +82,10 @@ def tile_svftrandompatternsingularcoupling_d1p_kernel(
                 src = scales[:, 4 * q : 4 * q + 4, :] if rows == 8 else scales[0, 4 * q : 4 * q + 4, :]
                 engine.dma_start(out=tile[32 * q : 32 * q + rows, :].bitcast(I32), in_=src.bitcast(I32))
 
+        warm = keep.tile([P, 16], F32, align_bytes=64, name="warm")
+        warmed = keep.tile([P, 16], F32, align_bytes=64, name="warmed")
+        nc.gpsimd.memset(warm[:], 0.0)
+        nc.scalar.copy(out=warmed[:], in_=warm[:])
         make_identity(nc, ident[:])
         nc.gpsimd.tensor_copy(
             out=pident[:].rearrange("p (t q b) -> p t q b", t=4, q=16),
@@ -93,16 +97,16 @@ def tile_svftrandompatternsingularcoupling_d1p_kernel(
         nc.sync.dma_start(out=xs[:], in_=x_scale.rearrange("(p i) j -> p (i j)", i=8))
         load_x(0, 1)
         load_x(1, 1)
-        load_scales(nc.scalar, us, u_scales, 8)
         for a in (0, 2):
             nc.sync.dma_start(out=pat[:, a : a + 2, :], in_=p_rows[:, a : a + 2, :])
             nc.sync.dma_start(out=mt[:, a : a + 2, :], in_=m_rows[:, a : a + 2, :])
-        load_scales(nc.sync, ws, w0_scales, 8)
         nc.sync.dma_start(out=ww[:, :, 0:512].bitcast(I32), in_=w_src[:, :, 0:512])
+        load_scales(nc.sync, ws, w0_scales, 8)
         load_x(2, 2)
         nc.sync.dma_start(out=uw[:].bitcast(I32), in_=u_src)
-        load_scales(nc.sync, vs, vt_scales, 4)
+        load_scales(nc.sync, us, u_scales, 8)
         nc.sync.dma_start(out=vw[:].bitcast(I32), in_=v_src)
+        load_scales(nc.sync, vs, vt_scales, 4)
         nc.sync.dma_start(out=ww[:, :, 512:1024].bitcast(I32), in_=w_src[:, :, 512:1024])
         load_x(4, 2)
         load_x(6, 2)
@@ -256,42 +260,63 @@ def tile_svftrandompatternsingularcoupling_d1p_kernel(
             live["hq", i] = (hq, hs)
             nc.vector.quantize_mx(out=hq[:].bitcast(X4), scales=hs[:], in_=live["hb", i][:])
 
-        def mm_b(i, h):
-            acc = bank("o")
-            live["o", i, h] = acc
-            cols = slice(512 * h, 512 * h + 512)
+        def sums(acc, i, cols, part):
+            hq, hs = live["hq", i] if part else (0, 0)
             for g in (0, 1):
+                if part < 2:
+                    nc.tensor.matmul_mx(
+                        out=acc,
+                        lhsT=xq[:, i, 128 * g : 128 * g + 128].bitcast(X4),
+                        lhsT_scale=xsc[:, i, 128 * g : 128 * g + 128],
+                        rhs=ww[:, g, cols].bitcast(X4),
+                        rhs_scale=ws[4 * g : P, cols],
+                        start=(g == 0),
+                        stop=False,
+                    )
+            if part:
                 nc.tensor.matmul_mx(
-                    out=acc[:],
-                    lhsT=xq[:, i, 128 * g : 128 * g + 128].bitcast(X4),
-                    lhsT_scale=xsc[:, i, 128 * g : 128 * g + 128],
-                    rhs=ww[:, g, cols].bitcast(X4),
-                    rhs_scale=ws[4 * g : P, cols],
-                    start=(g == 0),
-                    stop=False,
+                    out=acc,
+                    lhsT=hq[:].bitcast(X4),
+                    lhsT_scale=hs[:],
+                    rhs=nq[:, cols].bitcast(X4),
+                    rhs_scale=nsc[:, cols],
+                    start=False,
+                    stop=True,
                 )
 
+        def mm_b(i, h):
+            if (i, h) != (7, 0):
+                live["o", i, h] = bank("o")
+                sums(live["o", i, h][:], i, slice(512 * h, 512 * h + 512), 0)
+
         def mm_d(i, h):
-            hq, hs = live["hq", i]
-            nc.tensor.matmul_mx(
-                out=live["o", i, h][:],
-                lhsT=hq[:].bitcast(X4),
-                lhsT_scale=hs[:],
-                rhs=nq[:, 512 * h : 512 * h + 512].bitcast(X4),
-                rhs_scale=nsc[:, 512 * h : 512 * h + 512],
-                start=False,
-                stop=True,
-            )
+            if (i, h) != (7, 0):
+                sums(live["o", i, h][:], i, slice(512 * h, 512 * h + 512), 2)
+            else:
+                for k in (0, 1):
+                    acc = bank("o")
+                    live["o", i, h, k] = acc
+                    sums(acc[:, 0:256], i, slice(512 * h + 256 * k, 512 * h + 256 * k + 256), 1)
+
+        def store(i, cols, src):
+            nc.sync.dma_start(out=out_rows[:, i, cols], in_=src)
 
         def finish(i, h, eng):
-            osb = work.tile([P, 512], F32, align_bytes=64, name="osb", bufs=6)
-            acc = live["o", i, h]
+            osb = work.tile([P, 512], F32, align_bytes=64, name="osb", bufs=16)
             if i < 7:
-                copy(eng, osb[:], acc[:])
-            else:
+                copy(eng, osb[:], live["o", i, h][:])
+                store(i, slice(512 * h, 512 * h + 512), osb[:])
+            elif h != 0:
+                acc = live["o", i, h]
                 copy("s", osb[:, 0:256], acc[:, 0:256])
                 copy("v", osb[:, 256:512], acc[:, 256:512])
-            nc.sync.dma_start(out=out_rows[:, i, 512 * h : 512 * h + 512], in_=osb[:])
+                store(i, slice(512 * h, 512 * h + 512), osb[:])
+            else:
+                for k in (0, 1):
+                    acc = live["o", i, h, k]
+                    copy("s", osb[:, 256 * k : 256 * k + 128], acc[:, 0:128])
+                    copy("v", osb[:, 256 * k + 128 : 256 * k + 256], acc[:, 128:256])
+                    store(i, slice(512 * h + 256 * k, 512 * h + 256 * k + 256), osb[:, 256 * k : 256 * k + 256])
 
         steps = {
             "Wa": lambda i, e: widen(i, 0, e),

from contextlib import ExitStack

import concourse.mybir as mybir
from concourse.masks import make_identity

T, D, R, N = 1024, 1024, 512, 1024
FLOPS = 2 * (R * R * N + T * D * R + T * R * N + T * D * N)

P = 128
F32 = mybir.dt.float32
BF16 = mybir.dt.bfloat16
I32 = mybir.dt.int32
U32 = mybir.dt.uint32
U8 = mybir.dt.uint8
FP8 = mybir.dt.float8_e4m3fn
X4 = mybir.dt.float8_e4m3fn_x4
ALU = mybir.AluOpType
ACT = mybir.ActivationFunctionType

ORDER = (
    "Wa.0.v Wb.0.s Wa.1.v Wb.1.v Ma.0.- T.0.- C.0.v Ma.1.- Mb.0.- Mb.1.- Q.0.- T.1.- Tm.0.- C.1.s Wb.2.s "
    "Tm.1.- Cm.0.s Cm.1.s Wa.2.v Q.1.- Wb.3.v Ba.0.- T.2.- C.2.s Wa.3.v T.3.- Qm.0.- C.3.s UP.0.- Ba.1.- "
    "N.0.- Q.2.- N.1.- N.2.- CN.0.s CN.1.v Q.3.- CN.2.s H.0.- N.3.- H.1.- D.0.s Wa.4.v Wa.5.v N.4.- "
    "CN.3.s N.5.- QN.0.- QN.1.- I.0.- Wb.4.v D.1.s Wb.5.v Bb.0.- I.1.- H.2.- CN.4.s CN.5.s Wb.6.v Wa.6.v "
    "H.3.- Wa.7.v N.6.- Ea.0.- Ea.1.- D.2.s Wb.7.v D.3.s CN.6.s N.7.- Ba.2.- T.4.- QN.2.- CN.7.s Oa.0.s "
    "T.5.- I.2.- T.6.- QN.3.- C.4.s C.5.v Oa.1.s Q.4.- C.6.v T.7.- Ea.2.- Bb.1.- Eb.0.- Bb.2.- Eb.1.- "
    "Ob.0.v H.4.- Oa.2.v Eb.2.- Ob.1.v Bb.3.- I.3.- Ba.3.- Eb.3.- D.4.s Q.5.- I.4.- Bb.4.- Ea.3.- Q.6.- "
    "Ob.2.s H.5.- C.7.s Ba.4.- Oa.3.s Q.7.- Ob.3.v Eb.4.- D.5.v H.6.- Ea.4.- Bb.5.- Ba.5.- I.5.- Ob.4.v "
    "D.6.s Eb.5.- H.7.- I.6.- Ba.6.- Oa.4.s D.7.s Ob.5.v Ea.5.- Bb.6.- Oa.5.s Ea.6.- Eb.6.- Ob.6.s Bb.7.- "
    "I.7.- Oa.6.v Eb.7.- Ob.7.s Ba.7.- Ea.7.- Oa.7.v"
)


def tile_svftrandompatternsingularcoupling_d1p_kernel(
    tc, x_bytes, x_scale, w0_words, w0_scales, u_words, u_scales, m, pattern, vt_words, vt_scales, out
):
    nc = tc.nc
    with ExitStack() as ctx:
        keep = ctx.enter_context(tc.tile_pool(name="keep", bufs=1))
        work = ctx.enter_context(tc.tile_pool(name="work", bufs=8))
        psum = ctx.enter_context(tc.psum_pool(name="psum", bufs=1))

        xb = keep.tile([P, 8, D], U8, align_bytes=64, name="xb")
        xs = keep.tile([P, 64], F32, align_bytes=64, name="xs")
        pat = keep.tile([P, 4, R], BF16, align_bytes=64, name="pat")
        mt = keep.tile([P, 4, R], BF16, align_bytes=64, name="mt")
        msk = keep.tile([P, 4, R], BF16, align_bytes=64, name="msk")
        uw = keep.tile([P, 2, R], U32, align_bytes=64, name="uw")
        up = keep.tile([P, 2, R], U32, align_bytes=64, name="up")
        us = keep.tile([P, R], U8, align_bytes=64, name="us")
        usp = keep.tile([P, R], U8, align_bytes=64, name="usp")
        vw = keep.tile([P, N], U32, align_bytes=64, name="vw")
        vs = keep.tile([P, N], U8, align_bytes=64, name="vs")
        ww = keep.tile([P, 2, N], U32, align_bytes=64, name="ww")
        ws = keep.tile([P, N], U8, align_bytes=64, name="ws")
        ident = keep.tile([P, P], F32, align_bytes=64, name="ident")
        pident = keep.tile([P, P], F32, align_bytes=64, name="pident")
        msb = keep.tile([P, 2048], BF16, align_bytes=64, name="msb")
        msq = keep.tile([P, R], U32, align_bytes=64, name="msq")
        mss = keep.tile([P, R], U8, align_bytes=64, name="mss")
        nb = keep.tile([P, 4 * N], BF16, align_bytes=64, name="nb")
        nq = keep.tile([P, N], U32, align_bytes=64, name="nq")
        nsc = keep.tile([P, N], U8, align_bytes=64, name="nsc")
        xq = keep.tile([P, 8, 256], U32, align_bytes=64, name="xq")
        xsc = keep.tile([P, 8, 256], U8, align_bytes=64, name="xsc")

        ctx.enter_context(tc.manual_schedule())

        x_rows = x_bytes.rearrange("(p i) k -> p i k", i=8)
        m_rows = m.rearrange("(p a) k -> p a k", a=4)
        p_rows = pattern.rearrange("(p a) k -> p a k", a=4)
        out_rows = out.rearrange("(p i) n -> p i n", i=8)
        u_src = u_words.rearrange("g p n t -> p g (n t)").bitcast(I32)
        w_src = w0_words.rearrange("g p n t -> p g (n t)").bitcast(I32)
        v_src = vt_words[0].rearrange("p n t -> p (n t)").bitcast(I32)

        def load_x(i, count):
            nc.sync.dma_start(out=xb[:, i : i + count, :], in_=x_rows[:, i : i + count, :])

        def load_scales(engine, tile, scales, rows):
            for q in range(4):
                src = scales[:, 4 * q : 4 * q + 4, :] if rows == 8 else scales[0, 4 * q : 4 * q + 4, :]
                engine.dma_start(out=tile[32 * q : 32 * q + rows, :].bitcast(I32), in_=src.bitcast(I32))

        warm = keep.tile([P, 16], F32, align_bytes=64, name="warm")
        warmed = keep.tile([P, 16], F32, align_bytes=64, name="warmed")
        nc.gpsimd.memset(warm[:], 0.0)
        nc.scalar.copy(out=warmed[:], in_=warm[:])
        make_identity(nc, ident[:])
        nc.gpsimd.tensor_copy(
            out=pident[:].rearrange("p (t q b) -> p t q b", t=4, q=16),
            in_=ident[:].rearrange("p (q t b) -> p t q b", q=16, t=4),
        )
        nc.vector.memset(us[:].bitcast(I32), 0)
        nc.vector.memset(vs[:].bitcast(I32), 0)
        nc.vector.memset(ws[:].bitcast(I32), 0)
        nc.sync.dma_start(out=xs[:], in_=x_scale.rearrange("(p i) j -> p (i j)", i=8))
        load_x(0, 1)
        load_x(1, 1)
        for a in (0, 2):
            nc.sync.dma_start(out=pat[:, a : a + 2, :], in_=p_rows[:, a : a + 2, :])
            nc.sync.dma_start(out=mt[:, a : a + 2, :], in_=m_rows[:, a : a + 2, :])
        nc.sync.dma_start(out=ww[:, :, 0:512].bitcast(I32), in_=w_src[:, :, 0:512])
        load_scales(nc.sync, ws, w0_scales, 8)
        load_x(2, 2)
        nc.sync.dma_start(out=uw[:].bitcast(I32), in_=u_src)
        load_scales(nc.sync, us, u_scales, 8)
        nc.sync.dma_start(out=vw[:].bitcast(I32), in_=v_src)
        load_scales(nc.sync, vs, vt_scales, 4)
        nc.sync.dma_start(out=ww[:, :, 512:1024].bitcast(I32), in_=w_src[:, :, 512:1024])
        load_x(4, 2)
        load_x(6, 2)

        live = {}
        turn = {"r": 0, "o": 0}

        def bank(ring):
            turn[ring] = (turn[ring] + 1) % 4
            return psum.tile([P, 512], F32, tag="%s%d" % (ring, turn[ring]), name="bank")

        def widen(i, half, eng):
            if ("xw", i) not in live:
                live["xw", i] = work.tile([P, D], BF16, align_bytes=64, name="xw")
            live["split", i, half] = eng == "v"
            xw = live["xw", i]
            pairs = xw[:, 512 * half : 512 * half + 512].rearrange("p (u c e) -> p c u e", u=2, e=2)
            for b in range(4):
                j = 4 * half + b
                src = xb[:, i, 128 * j : 128 * j + 128].bitcast(FP8)
                sc = xs[:, 8 * i + j : 8 * i + j + 1]
                if eng == "v":
                    nc.vector.tensor_scalar(
                        out=pairs[:, 32 * b : 32 * b + 32, :, :],
                        in0=src.rearrange("p (c u e) -> p c u e", u=2, e=2),
                        scalar1=sc,
                        scalar2=None,
                        op0=ALU.mult,
                    )
                else:
                    nc.scalar.activation(out=xw[:, 128 * j : 128 * j + 128], in_=src, func=ACT.Copy, scale=sc)

        def turn_x(i):
            tr = bank("r")
            live["tr", i] = tr
            words = live["xw", i][:].bitcast(F32)
            for g in (0, 1):
                for u in (0, 1):
                    c = 128 * (2 * g + u)
                    if live["split", i, g]:
                        src = words[:, 256 * g + 128 * u : 256 * g + 128 * u + 128]
                    else:
                        src = words[:, 256 * g + u : 256 * g + 256 : 2]
                    nc.tensor.transpose(tr[:, c : c + 128], src, ident[:])

        def copy(eng, dst, src):
            if eng == "v":
                nc.vector.tensor_copy(out=dst, in_=src)
            else:
                nc.scalar.copy(out=dst, in_=src)

        def copy_x(i, eng):
            xg = work.tile([P, D], BF16, align_bytes=64, name="xg")
            live["xg", i] = xg
            copy(
                eng,
                xg[:].bitcast(F32).rearrange("p (g c u) -> p g c u", g=2, u=2),
                live["tr", i][:].rearrange("p (g u c) -> p g c u", g=2, u=2),
            )

        def quant_x(i):
            nc.vector.quantize_mx(out=xq[:, i, :].bitcast(X4), scales=xsc[:, i, :], in_=live["xg", i][:])

        def permute_u():
            for g in (0, 1):
                nc.vector.tensor_copy(
                    out=up[:, g, :].bitcast(I32).rearrange("p (t q j) -> p t q j", t=4, q=16),
                    in_=uw[:, g, :].bitcast(I32).rearrange("p (q t j) -> p t q j", q=16, t=4),
                )
            nc.vector.tensor_copy(
                out=usp[:].bitcast(I32).rearrange("p (t q j) -> p t q j", t=4, q=16),
                in_=us[:].bitcast(I32).rearrange("p (q t j) -> p t q j", q=16, t=4),
            )

        def mask_a(h):
            a = slice(2 * h, 2 * h + 2)
            nc.vector.tensor_scalar(out=msk[:, a, :], in0=pat[:, a, :], scalar1=0.25, scalar2=None, op0=ALU.is_lt)

        def mask_b(h):
            a = slice(2 * h, 2 * h + 2)
            nc.vector.tensor_tensor(out=msk[:, a, :], in0=msk[:, a, :], in1=mt[:, a, :], op=ALU.mult)

        def turn_m(h):
            tr = bank("r")
            live["trm", h] = tr
            for e in (0, 1):
                words = msk[:, 2 * h + e, :].bitcast(F32)
                for u in (0, 1):
                    c = 128 * (2 * e + u)
                    nc.tensor.transpose(tr[:, c : c + 128], words[:, u:256:2], pident[:])

        def copy_m(h, eng):
            dst = msb[:].bitcast(F32).rearrange("p (c a u) -> p c a u", a=4, u=2)[:, :, 2 * h : 2 * h + 2, :]
            copy(eng, dst, live["trm", h][:].rearrange("p (a u c) -> p c a u", a=2, u=2))

        def quant_m():
            nc.vector.quantize_mx(out=msq[:].bitcast(X4), scales=mss[:], in_=msb[:])

        def mm_n(c):
            acc = bank("r")
            live["n", c] = acc
            cols = slice(128 * c, 128 * c + 128)
            for t in range(4):
                nc.tensor.matmul_mx(
                    out=acc[:, 128 * t : 128 * t + 128],
                    lhsT=msq[:, 128 * t : 128 * t + 128].bitcast(X4),
                    lhsT_scale=mss[:, 128 * t : 128 * t + 128],
                    rhs=vw[:, cols].bitcast(X4),
                    rhs_scale=vs[:, cols],
                    start=True,
                    stop=True,
                )

        def copy_n(c, eng):
            copy(
                eng,
                nb[:, 512 * c : 512 * c + 512].rearrange("p (n t) -> p n t", t=4),
                live["n", c][:].rearrange("p (t n) -> p n t", t=4),
            )

        def quant_n(h):
            nc.vector.quantize_mx(
                out=nq[:, 256 * h : 256 * h + 256].bitcast(X4),
                scales=nsc[:, 256 * h : 256 * h + 256],
                in_=nb[:, 1024 * h : 1024 * h + 1024],
            )

        def mm_h(i):
            acc = bank("r")
            live["h", i] = acc
            for t in range(4):
                for g in (0, 1):
                    nc.tensor.matmul_mx(
                        out=acc[:, 128 * t : 128 * t + 128],
                        lhsT=up[:, g, 128 * t : 128 * t + 128].bitcast(X4),
                        lhsT_scale=usp[4 * g : P, 128 * t : 128 * t + 128],
                        rhs=xq[:, i, 128 * g : 128 * g + 128].bitcast(X4),
                        rhs_scale=xsc[:, i, 128 * g : 128 * g + 128],
                        start=(g == 0),
                        stop=(g == 1),
                    )

        def copy_h(i, eng):
            hb = work.tile([P, 512], BF16, align_bytes=64, name="hb")
            live["hb", i] = hb
            copy(eng, hb[:].rearrange("p (n t) -> p n t", t=4), live["h", i][:].rearrange("p (t n) -> p n t", t=4))

        def quant_h(i):
            hq = work.tile([P, P], U32, align_bytes=64, name="hq", bufs=8)
            hs = work.tile([P, P], U8, align_bytes=64, name="hs", bufs=8)
            live["hq", i] = (hq, hs)
            nc.vector.quantize_mx(out=hq[:].bitcast(X4), scales=hs[:], in_=live["hb", i][:])

        def sums(acc, i, cols, part):
            hq, hs = live["hq", i] if part else (0, 0)
            for g in (0, 1):
                if part < 2:
                    nc.tensor.matmul_mx(
                        out=acc,
                        lhsT=xq[:, i, 128 * g : 128 * g + 128].bitcast(X4),
                        lhsT_scale=xsc[:, i, 128 * g : 128 * g + 128],
                        rhs=ww[:, g, cols].bitcast(X4),
                        rhs_scale=ws[4 * g : P, cols],
                        start=(g == 0),
                        stop=False,
                    )
            if part:
                nc.tensor.matmul_mx(
                    out=acc,
                    lhsT=hq[:].bitcast(X4),
                    lhsT_scale=hs[:],
                    rhs=nq[:, cols].bitcast(X4),
                    rhs_scale=nsc[:, cols],
                    start=False,
                    stop=True,
                )

        def mm_b(i, h):
            if (i, h) != (7, 0):
                live["o", i, h] = bank("o")
                sums(live["o", i, h][:], i, slice(512 * h, 512 * h + 512), 0)

        def mm_d(i, h):
            if (i, h) != (7, 0):
                sums(live["o", i, h][:], i, slice(512 * h, 512 * h + 512), 2)
            else:
                for k in (0, 1):
                    acc = bank("o")
                    live["o", i, h, k] = acc
                    sums(acc[:, 0:256], i, slice(512 * h + 256 * k, 512 * h + 256 * k + 256), 1)

        def store(i, cols, src):
            nc.sync.dma_start(out=out_rows[:, i, cols], in_=src)

        def finish(i, h, eng):
            osb = work.tile([P, 512], F32, align_bytes=64, name="osb", bufs=16)
            if i < 7:
                copy(eng, osb[:], live["o", i, h][:])
                store(i, slice(512 * h, 512 * h + 512), osb[:])
            elif h != 0:
                acc = live["o", i, h]
                copy("s", osb[:, 0:256], acc[:, 0:256])
                copy("v", osb[:, 256:512], acc[:, 256:512])
                store(i, slice(512 * h, 512 * h + 512), osb[:])
            else:
                for k in (0, 1):
                    acc = live["o", i, h, k]
                    copy("s", osb[:, 256 * k : 256 * k + 128], acc[:, 0:128])
                    copy("v", osb[:, 256 * k + 128 : 256 * k + 256], acc[:, 128:256])
                    store(i, slice(512 * h + 256 * k, 512 * h + 256 * k + 256), osb[:, 256 * k : 256 * k + 256])

        steps = {
            "Wa": lambda i, e: widen(i, 0, e),
            "Wb": lambda i, e: widen(i, 1, e),
            "T": lambda i, e: turn_x(i),
            "C": copy_x,
            "Q": lambda i, e: quant_x(i),
            "UP": lambda i, e: permute_u(),
            "Ma": lambda i, e: mask_a(i),
            "Mb": lambda i, e: mask_b(i),
            "Tm": lambda i, e: turn_m(i),
            "Cm": copy_m,
            "Qm": lambda i, e: quant_m(),
            "N": lambda i, e: mm_n(i),
            "CN": copy_n,
            "QN": lambda i, e: quant_n(i),
            "H": lambda i, e: mm_h(i),
            "D": copy_h,
            "I": lambda i, e: quant_h(i),
            "Ba": lambda i, e: mm_b(i, 0),
            "Bb": lambda i, e: mm_b(i, 1),
            "Ea": lambda i, e: mm_d(i, 0),
            "Eb": lambda i, e: mm_d(i, 1),
            "Oa": lambda i, e: finish(i, 0, e),
            "Ob": lambda i, e: finish(i, 1, e),
        }
        for step in ORDER.split(" "):
            kind, index, engine = step.split(".")
            steps[kind](int(index), engine)
